import numpy as np
import ml_dtypes


def mxq(x, axis, fmt="e4m3"):
    dtype, down = {"e4m3": (ml_dtypes.float8_e4m3fn, 7), "e5m2": (ml_dtypes.float8_e5m2, 14)}[fmt]
    v = np.moveaxis(np.asarray(x, np.float32).astype(ml_dtypes.bfloat16).astype(np.float64), axis, -1)
    blocks = v.reshape(v.shape[:-1] + (-1, 32))
    amax = np.abs(blocks).max(-1, keepdims=True)
    byte = np.maximum(np.where(amax > 0, np.frexp(amax)[1] - 1 + 127, 0) - down, 1)
    scale = np.exp2(byte - 127.0)
    codes = (blocks / scale).astype(np.float32).astype(dtype).astype(np.float64)
    return np.moveaxis((codes * scale).reshape(v.shape), -1, axis)


WIDE = False


def mx_kscale(k):
    if not WIDE:
        return np.ones(k)
    levels = np.array([10, -10, 5, -5, 0])
    if k % 512:
        return np.exp2(np.random.permutation(np.resize(levels, k // 32))).repeat(32)
    a = np.empty((k // 512, 16))
    for p in range(k // 512):
        a[p, :8] = np.random.permutation(np.resize(levels, 8))
        for g in range(8):
            far = levels[np.abs(levels - a[p, g]) >= 10]
            a[p, g + 8] = far[np.random.randint(len(far))]
    return np.exp2(a.ravel()).repeat(32)


BF16 = ml_dtypes.bfloat16


def bf(x):
    return np.asarray(x, np.float32).astype(BF16)


def f64(x):
    return np.asarray(x).astype(np.float64)


H, W, D, F = 2, 1024, 512, 512
P = 2
L = W + W // P
DISP_STEP = 128.0
WIDTH0 = 128.0
WIDTH1 = 256.0


def scanline_correlation(f_left, f_right):
    d = f_left.shape[-1]
    prod = mxq(f_left, 2, "e4m3") @ mxq(f_right, 2, "e4m3").transpose(0, 2, 1)
    return prod / np.sqrt(d)


def pool_pairs(corr):
    h, w, n = corr.shape
    return np.mean(corr.reshape(h, w, n // P, P), axis=-1)


def gaussian_window(pos, ctr, width):
    t = (pos[None, None, :] - ctr[:, :, None]) / width
    return np.exp(-0.5 * t ** 2)


def draw0():
    s, t = mx_kscale(D), mx_kscale(L)
    return {
        "f_left": bf(np.random.standard_normal((H, W, D)) * s),
        "f_right": bf(np.random.standard_normal((H, W, D)) / s),
        "disp": bf(np.random.uniform(0.0, 2.0, (H, W))),
        "gain": bf((1.0 + 0.1 * np.random.standard_normal(L)) * t),
        "w_corr": bf(np.random.standard_normal((L, F)) * 3.135 / np.sqrt(L) / t[:, None]),
        "w_disp": bf(np.random.standard_normal(F)),
        "b_mot": bf(np.random.standard_normal(F) * 0.3),
    }


def core(f_left, f_right, disp, gain, w_corr, w_disp, b_mot):
    f_left, f_right, disp, gain = f64(f_left), f64(f_right), f64(disp), f64(gain)
    w_corr, w_disp, b_mot = f64(w_corr), f64(w_disp), f64(b_mot)
    w = f_left.shape[1]

    corr = scanline_correlation(f_left, f_right)

    half = pool_pairs(corr)

    i = np.arange(w, dtype=np.float64)
    ctr = i[None, :] - DISP_STEP * disp

    j0 = np.arange(w, dtype=np.float64)
    j1 = np.arange(w // P, dtype=np.float64)
    win0 = gaussian_window(j0, ctr, WIDTH0)
    win1 = gaussian_window(2.0 * j1 + 0.5, ctr, WIDTH1)

    c = np.concatenate([win0 * corr, win1 * half], axis=-1)

    cg = c * gain

    pre = (mxq(cg, 2, "e4m3") @ mxq(w_corr, 0, "e4m3")) + (disp - 1.0)[..., None] * w_disp + b_mot
    return np.maximum(pre, 0.0)


def e4m3fn_bytes(y):
    return np.clip(np.asarray(y, np.float64), -448.0, 448.0).astype(np.float32).astype(ml_dtypes.float8_e4m3fn).view(np.uint8)


def e4m3fn_values(b):
    return np.asarray(b, np.uint8).view(ml_dtypes.float8_e4m3fn).astype(np.float64)


def setup_inputs():
    d = draw0()
    x0 = np.asarray(d['f_right']).astype(np.float64)
    s = (np.max(np.abs(x0), axis=(0, 1), keepdims=True) / 448.0).astype(np.float32)
    out = {}
    for k, v in d.items():
        if k == 'f_right':
            out['f_right_bytes'] = e4m3fn_bytes(x0 / s.astype(np.float64))
            out['f_right_scale'] = s
        else:
            out[k] = v
    return out


def reference(f_left, f_right_bytes, f_right_scale, disp, gain, w_corr, w_disp, b_mot):
    return core(f_left, e4m3fn_values(f_right_bytes) * f_right_scale.astype(np.float64), disp, gain, w_corr, w_disp, b_mot)

import math
from contextlib import ExitStack

import concourse.mybir as mybir
from concourse.masks import make_identity

F32 = mybir.dt.float32
BF16 = mybir.dt.bfloat16
U32 = mybir.dt.uint32
U8 = mybir.dt.uint8
FP8 = mybir.dt.float8_e4m3fn
FP8X4 = mybir.dt.float8_e4m3fn_x4
ALU = mybir.AluOpType
ACT = mybir.ActivationFunctionType

P = 128
H, W, D, F = 2, 1024, 512, 512
L = W + W // 2
MB = W // P
FLOPS = 2 * H * W * W * D + 2 * H * W * L * F

STEP = 128.0
S0 = 128.0
S1 = 256.0
CENTRE = 512.0
FAR = 16384.0
TINY = 2.0 ** -60
HUGE = 2.0 ** 60
HALF_LN_D = 0.5 * math.log(D)
LN2 = math.log(2.0)
KR = 24
WIN_BUFS = 2


def tile_stereocorrpyramidmotionencoder_kernel(
    tc, f_left, f_right_bytes, f_right_scale, disp, gain, w_corr, w_disp, b_mot, out
):
    nc = tc.nc
    with ExitStack() as ctx:
        const = ctx.enter_context(tc.tile_pool(name="const", bufs=1))
        work = ctx.enter_context(tc.tile_pool(name="work", bufs=1))
        psum = ctx.enter_context(tc.psum_pool(name="psum", bufs=1))

        def bank(tag, bufs, dtype=F32):
            t = psum.tile([P, 4, P], dtype, tag=tag, bufs=bufs, name=tag)
            return t

        def misc(dtype=F32):
            return bank("misc", 3, dtype)

        ctx.enter_context(tc.manual_schedule())

        g0_raw = const.tile([P, 2, 4], BF16)
        nc.scalar.dma_start(out=g0_raw[:], in_=gain[0:W].rearrange("(G p t) -> p G t", G=2, t=4))
        g1_raw = const.tile([P, 2, 2], BF16)
        nc.scalar.dma_start(out=g1_raw[:], in_=gain[W:L].rearrange("(G p t) -> p G t", G=2, t=2))
        s4 = const.tile([P, 4], F32)
        nc.sync.dma_start(out=s4[:], in_=f_right_scale.rearrange("a b (p m) -> p (a b m)", m=4))
        d_raw = const.tile([P, H, MB], BF16)
        nc.scalar.dma_start(out=d_raw[:], in_=disp.rearrange("y (p m) -> p y m", m=MB))
        wd4 = const.tile([P, 4], BF16)
        nc.scalar.dma_start(out=wd4[:], in_=w_disp.rearrange("(p m) -> p m", m=4))
        bm4 = const.tile([P, 4], BF16)
        nc.scalar.dma_start(out=bm4[:], in_=b_mot.rearrange("(p m) -> p m", m=4))

        fr_raw, fl_raw = [], []
        w_sb = const.tile([P, 12, F], BF16)
        for y in range(H):
            fr = const.tile([P, 2, 4, D], U8, name="fr_raw%d" % y)
            nc.sync.dma_start(out=fr[:], in_=f_right_bytes[y].rearrange("(G p t) d -> p G t d", G=2, t=4))
            fr_raw.append(fr)
            fl = const.tile([P, MB, D], BF16, name="fl_raw%d" % y)
            fl_rows = f_left[y].rearrange("(p m) d -> p m d", m=MB)
            fl_raw.append(fl)
            nc.sync.dma_start(out=fl[:, 0:4, :], in_=fl_rows[:, 0:4, :])
            if y == 0:
                w0 = w_corr[0:W].rearrange("(q g r t) f -> r q g t f", g=2, r=8, t=4)
                w1 = w_corr[W:L].rearrange("(q g r t) f -> r q g t f", g=2, r=8, t=2)
                for r in range(8):
                    nc.sync.dma_start(
                        out=w_sb[r:P:8, 0:8, :].rearrange("q (g t) f -> q g (t f)", g=2),
                        in_=w0[r].rearrange("q g t f -> q g (t f)"),
                    )
                for r in range(8):
                    nc.sync.dma_start(
                        out=w_sb[r:P:8, 8:12, :].rearrange("q (g t) f -> q g (t f)", g=2),
                        in_=w1[r].rearrange("q g t f -> q g (t f)"),
                    )

            nc.sync.dma_start(out=fl[:, 4:8, :], in_=fl_rows[:, 4:8, :])

        gt = const.tile([P, 16 + P], F32)
        nc.vector.memset(gt[:], 0.0)
        a_src = const.tile([P, 8, P], BF16)
        nc.vector.memset(a_src[:], 0.0)
        ident = const.tile([P, P], F32)
        make_identity(nc, ident[:])
        ident_b = const.tile([P, P], BF16)
        nc.vector.tensor_copy(out=ident_b[:], in_=ident[:])
        bt = const.tile([P, H * MB * KR + P], BF16)
        nc.vector.memset(bt[:], 0.0)
        gtv = gt[:, 0:32].rearrange("p (G c) -> p G c", G=2)
        nc.gpsimd.iota(gtv[:, :, 8:12], pattern=[[512, 2], [1, 4]], base=-int(CENTRE), channel_multiplier=4,
                       allow_small_or_imprecise_dtypes=True)
        pos = const.tile([P, H, MB], F32)
        nc.gpsimd.iota(pos[:], pattern=[[0, H], [1, MB]], base=-int(CENTRE), channel_multiplier=MB,
                       allow_small_or_imprecise_dtypes=True)
        nc.gpsimd.iota(a_src[:, :, 16:19].rearrange("p (g t) k -> p g t k", g=2), pattern=[[0, 2], [1, 4], [0, 3]], base=0,
                       channel_multiplier=0, allow_small_or_imprecise_dtypes=True)
        nc.gpsimd.memset(a_src[:, :, 19:22], 1.0)

        def spread(vec4, name, copy):
            dt, one = (F32, ident) if vec4.dtype == F32 else (BF16, ident_b)
            ps = misc(dt)
            for m in range(4):
                nc.tensor.transpose(ps[:, m, :], vec4[:, m : m + 1].to_broadcast([P, P]), one[:])
            row = const.tile([P, 4 * P], F32, name=name)
            copy(out=row[:].rearrange("p (n m) -> p n m", m=4), in_=ps[:].rearrange("p m n -> p n m"))
            return row

        s_bc = spread(s4, "s_bc", nc.scalar.copy)

        nc.vector.tensor_copy(out=gtv[:, :, 0:4], in_=g0_raw[:])
        nc.vector.tensor_copy(out=gtv[:, :, 4:6], in_=g1_raw[:])
        t1 = misc()
        for G in range(2):
            nc.tensor.transpose(t1[:, G, :], gt[:, 16 * G : 16 * G + P], ident[:])
        s1 = const.tile([P, 2, P], F32)
        nc.vector.tensor_copy(
            out=s1[:].rearrange("p g (Q r) -> p g Q r", r=8),
            in_=t1[:, 0:2, :].rearrange("p G (q g r) -> p g (G q) r", g=2, r=8),
        )
        t2 = misc()
        for g in range(2):
            nc.tensor.transpose(t2[:, g, :], s1[:, g, :], ident[:])
        gp = const.tile([P, 2, 12], F32)
        mag = const.tile([P, 2, 6], F32)
        mag2 = const.tile([P, 2, 6], F32)
        lng = const.tile([P, 2, 6], F32)
        jsq = const.tile([P, 2, 4], F32)
        jsq2 = const.tile([P, 2, 4], F32)
        tt = const.tile([P, 2, 4], F32)
        tr1 = const.tile([P, 2, 4], F32)
        tr2 = const.tile([P, 2, 4], F32)
        bias1 = const.tile([P, 2, 2], F32)
        pos1 = const.tile([P, 2, 2], F32)
        sgn_h = const.tile([P, 2, 6], F32)
        sgn = const.tile([P, 2, 6], F32)
        av = a_src[:].rearrange("p (g t) k -> p g t k", g=2)

        def piece(k):
            return av[:, :, :, 3 + k]

        gain_steps = [
            lambda: nc.vector.tensor_copy(out=gp[:], in_=t2[:, 0:2, 0:12]),
            lambda: nc.vector.scalar_tensor_tensor(out=mag[:], in0=gp[:, :, 0:6], scalar=-1.0, in1=gp[:, :, 0:6], op0=ALU.mult, op1=ALU.max),
            lambda: nc.vector.tensor_scalar(out=mag2[:], in0=mag[:], scalar1=TINY, scalar2=HUGE, op0=ALU.max, op1=ALU.min),
            lambda: nc.scalar.activation(out=lng[:], in_=mag2[:], func=ACT.Ln),
            lambda: nc.gpsimd.tensor_scalar(out=sgn_h[:], in0=gp[:, :, 0:6], scalar1=0.0, scalar2=2.0, op0=ALU.is_ge, op1=ALU.mult),
            lambda: nc.gpsimd.tensor_scalar(out=sgn[:], in0=sgn_h[:], scalar1=1.0, scalar2=-1.0, op0=ALU.mult, op1=ALU.add),
            lambda: nc.vector.scalar_tensor_tensor(out=jsq[:], in0=gp[:, :, 8:12], scalar=-0.5, in1=gp[:, :, 8:12], op0=ALU.mult, op1=ALU.mult),
            lambda: nc.vector.tensor_copy(out=av[:, :, :, 0:3], in_=gp[:, :, 8:9].unsqueeze(3).to_broadcast([P, 2, 4, 3])),
            lambda: nc.vector.tensor_scalar(out=jsq2[:], in0=jsq[:], scalar1=-HALF_LN_D * S0 * S0, scalar2=None, op0=ALU.add),
            lambda: nc.vector.tensor_scalar(out=pos1[:], in0=gp[:, :, 8:12:2], scalar1=0.5, scalar2=-1.0 / (S1 * math.sqrt(2.0)), op0=ALU.add, op1=ALU.mult),
            lambda: nc.vector.scalar_tensor_tensor(out=tt[:], in0=lng[:, :, 0:4], scalar=S0 * S0, in1=jsq2[:], op0=ALU.mult, op1=ALU.add),
            lambda: nc.vector.tensor_scalar(out=bias1[:], in0=lng[:, :, 4:6], scalar1=-(HALF_LN_D + LN2), scalar2=None, op0=ALU.add),
            lambda: nc.vector.tensor_copy(out=piece(0), in_=tt[:]),
            lambda: nc.vector.tensor_tensor(out=tr1[:], in0=tt[:], in1=piece(0), op=ALU.subtract),
            lambda: nc.vector.tensor_copy(out=piece(1), in_=tr1[:]),
            lambda: nc.vector.tensor_tensor(out=tr2[:], in0=tr1[:], in1=piece(1), op=ALU.subtract),
            lambda: nc.vector.tensor_copy(out=piece(2), in_=tr2[:]),
        ]

        c_sh = const.tile([P, H * MB], F32)
        draw = d_raw[:].rearrange("p y m -> p (y m)")
        nc.gpsimd.tensor_scalar(out=c_sh[:], in0=draw, scalar1=-STEP, scalar2=0.0, op0=ALU.mult, op1=ALU.add)
        c_un = const.tile([P, H * MB], F32)
        nc.gpsimd.tensor_tensor(out=c_un[:], in0=c_sh[:], in1=pos[:].rearrange("p y m -> p (y m)"), op=ALU.add)
        cq = const.tile([P, 2, H * MB], F32)
        nc.gpsimd.tensor_scalar(out=cq[:, 0, :], in0=c_un[:], scalar1=FAR, scalar2=-FAR, op0=ALU.min, op1=ALU.max)
        csq = const.tile([P, H * MB], F32)
        nc.gpsimd.tensor_tensor(out=csq[:], in0=cq[:, 0, :], in1=cq[:, 0, :], op=ALU.mult)
        nc.gpsimd.tensor_scalar(out=cq[:, 1, :], in0=csq[:], scalar1=-0.5, scalar2=0.0, op0=ALU.mult, op1=ALU.add)
        c3 = const.tile([P, 3, 2, H * MB], BF16)
        nc.gpsimd.tensor_copy(out=c3[:, 0], in_=cq[:])
        r1 = const.tile([P, 2, H * MB], F32)
        nc.gpsimd.tensor_tensor(out=r1[:], in0=cq[:], in1=c3[:, 0], op=ALU.subtract)
        nc.gpsimd.tensor_copy(out=c3[:, 1], in_=r1[:])
        r2 = const.tile([P, 2, H * MB], F32)
        nc.gpsimd.tensor_tensor(out=r2[:], in0=r1[:], in1=c3[:, 1], op=ALU.subtract)
        nc.gpsimd.tensor_copy(out=c3[:, 2], in_=r2[:])
        btv = bt[:, 0 : H * MB * KR].rearrange("p (b k) -> p b k", k=KR)
        nc.gpsimd.memset(btv[:, :, 3:6], 1.0)
        nc.gpsimd.tensor_copy(out=btv[:, :, 0:3], in_=c3[:, :, 0, :].rearrange("p k b -> p b k"))
        nc.gpsimd.tensor_copy(out=btv[:, :, 16:19], in_=c3[:, :, 0, :].rearrange("p k b -> p b k"))
        nc.gpsimd.tensor_copy(out=btv[:, :, 19:22], in_=c3[:, :, 1, :].rearrange("p k b -> p b k"))
        dm1 = const.tile([P, H * MB], F32)
        nc.gpsimd.tensor_scalar(out=dm1[:], in0=draw, scalar1=1.0, scalar2=-1.0, op0=ALU.mult, op1=ALU.add)

        rh = const.tile([P, H * MB, P], BF16)
        at = const.tile([P, 8, P], BF16)

        def turn_slots(k):
            ps = misc(BF16)
            for s in range(4):
                nc.tensor.transpose(ps[:, s, :], a_src[:, 4 * k + s, :], ident_b[:])
            nc.scalar.copy(out=at[:, 4 * k : 4 * k + 4, :], in_=ps[:])

        def turn_pixels(k):
            ps = misc(BF16)
            for s in range(4):
                b = 4 * k + s
                nc.tensor.transpose(ps[:, s, :], bt[:, KR * b : KR * b + P], ident_b[:])
            nc.scalar.copy(out=rh[:, 4 * k : 4 * k + 4, :], in_=ps[:])

        frq, frs, flq, fls, frg = [], [], [], [], []
        for y in range(H):
            frq.append(const.tile([P, 8 * P], U32, name="frq%d" % y, align_bytes=64))
            frs.append(const.tile([P, 8 * P], U8, name="frs%d" % y, align_bytes=64))
            flq.append(const.tile([P, 8 * P], U32, name="flq%d" % y, align_bytes=64))
            fls.append(const.tile([P, 8 * P], U8, name="fls%d" % y, align_bytes=64))
            frg.append(const.tile([P, 8, P, 4], BF16, name="frg%d" % y, align_bytes=64))

        def widen(y, t, wide, G):
            nc.vector.tensor_tensor(out=wide[:, G, :], in0=fr_raw[y][:, G, t, :].bitcast(FP8), in1=s_bc[:], op=ALU.mult)

        def wide_tile():
            wide = work.tile([P, 2, D], BF16, tag="wide", bufs=3, name="wide")
            return wide

        def turn_right(y, t, wide):
            frg_words = frg[y][:].rearrange("p s c k -> p (s c k)").bitcast(F32).rearrange("p (g t n) -> p g t n", g=2, t=4)
            words = wide[:].rearrange("p G d -> p (G d)").bitcast(F32)
            ps = misc()
            for u in range(2):
                for G in range(2):
                    nc.tensor.transpose(ps[:, 2 * u + G, :], words[:, 256 * G + u : 256 * (G + 1) : 2], ident[:])
            src = ps[:].rearrange("p (u G) (q g r) -> p g (G q) r u", u=2, g=2, r=8)
            for g in range(2):
                nc.scalar.copy(out=frg_words[:, g, t, :].rearrange("p (Q r u) -> p Q r u", r=8, u=2), in_=src[:, g])

        def quantise_right(y, g):
            cols = slice(4 * P * g, 4 * P * (g + 1))
            nc.vector.quantize_mx(out=frq[y][:, cols].bitcast(FP8X4), scales=frs[y][:, cols],
                                  in_=frg[y][:, 4 * g : 4 * g + 4].rearrange("p s c k -> p (s c k)"))

        def turn_left(y, j):
            return copy_left(turn_left_mm(y, j))

        def turn_left_mm(y, j):
            words = fl_raw[y][:].rearrange("p m d -> p (m d)").bitcast(F32)
            ps = misc()
            for mm in range(2):
                m = 2 * j + mm
                for u in range(2):
                    nc.tensor.transpose(ps[:, 2 * mm + u, :], words[:, 256 * m + u : 256 * (m + 1) : 2], ident[:])
            return ps

        def copy_left(ps):
            flg = work.tile([P, 2, P, 4], BF16, tag="flg", bufs=2, name="flg", align_bytes=64)
            flg_words = flg[:].rearrange("p m c k -> p (m c k)").bitcast(F32).rearrange("p (m c u) -> p m c u", c=P, u=2)
            nc.scalar.copy(out=flg_words, in_=ps[:].rearrange("p (m u) c -> p m c u", u=2))
            return flg

        def quantise_left(y, j, flg):
            cols = slice(2 * P * j, 2 * P * (j + 1))
            nc.vector.quantize_mx(out=flq[y][:, cols].bitcast(FP8X4), scales=fls[y][:, cols],
                                  in_=flg[:].rearrange("p m c k -> p (m c k)"))

        wq = const.tile([P, 3, F], U32, align_bytes=64)
        ws = const.tile([P, 3, F], U8, align_bytes=64)
        wg = [const.tile([P, F, 4], BF16, name="wg%d" % k, align_bytes=64) for k in range(3)]

        def group_w(k):
            for n in range(4):
                fc = slice(P * n, P * (n + 1))
                if k < 2:
                    src, dst = w_sb[:, 4 * k : 4 * k + 4, fc].rearrange("p t f -> p f t"), wg[k][:, fc, :]
                    sg = sgn[:, k, 0:4].unsqueeze(1).to_broadcast([P, P, 4])
                else:
                    src = w_sb[:, 8:12, fc].rearrange("p (g t) f -> p f g t", g=2)
                    dst = wg[k][:, fc, :].rearrange("p f (g t) -> p f g t", g=2)
                    sg = sgn[:, :, 4:6].unsqueeze(1).to_broadcast([P, P, 2, 2])
                nc.gpsimd.tensor_tensor(out=dst, in0=src, in1=sg, op=ALU.mult)

        def quantise_w(k):
            nc.vector.quantize_mx(out=wq[:, k, :].bitcast(FP8X4), scales=ws[:, k, :], in_=wg[k][:].rearrange("p f t -> p (f t)"))

        def window0(y, m, g):
            e = bank("e", 2)
            for t in range(4):
                nc.tensor.matmul(e[:, t, :], lhsT=at[:, 4 * g + t, :], rhs=rh[:, MB * y + m, :], start=True, stop=True)
            return e

        def exp0(e):
            win = work.tile([P, P, 4], F32, tag="win0", bufs=WIN_BUFS * 4, name="win0")
            nc.scalar.activation(out=win[:], in_=e[:].rearrange("p t n -> p n t"), func=ACT.Exp, scale=1.0 / (S0 * S0))
            return win

        def centres(y, j):
            ps = misc()
            for mm in range(2):
                b = MB * y + 2 * j + mm
                nc.tensor.transpose(ps[:, mm, :], cq[:, 0, b : b + 1].to_broadcast([P, P]), ident[:])
            win = work.tile([P, 4, 2 * P], F32, tag="win1", bufs=WIN_BUFS, name="win1")
            return ps, win

        def square1(ps, s):
            sq = work.tile([P, 2 * P], F32, tag="sq", bufs=4, name="sq")
            nc.scalar.activation(out=sq[:], in_=ps[:, 0:2, :].rearrange("p m n -> p (m n)"), func=ACT.Square,
                                 bias=pos1[:, s // 2, s % 2 : s % 2 + 1], scale=1.0 / (S1 * math.sqrt(2.0)))
            return sq

        def exp1(win, sq, s):
            nc.scalar.activation(out=win[:, s, :], in_=sq[:], func=ACT.Exp, bias=bias1[:, s // 2, s % 2 : s % 2 + 1], scale=-1.0)

        def correlate(y, m, lhs_slots):
            ps = bank("corr", 3)
            cols = slice(P * m, P * (m + 1))
            for s in range(4):
                for i, slot in enumerate(lhs_slots[s]):
                    rows = slice(P * slot, P * (slot + 1))
                    nc.tensor.matmul_mx(out=ps[:, s, :], lhsT=frq[y][:, rows].bitcast(FP8X4), lhsT_scale=frs[y][:, rows],
                                        rhs=flq[y][:, cols].bitcast(FP8X4), rhs_scale=fls[y][:, cols],
                                        start=(i == 0), stop=(i == len(lhs_slots[s]) - 1))
            return ps

        SLOTS = [[(t,) for t in range(4)], [(4 + t,) for t in range(4)], [(2 * s, 2 * s + 1) for s in range(4)]]

        def quantise_taps(cg):
            cgq = work.tile([P, 2 * P], U32, tag="cgq", bufs=12, name="cgq", align_bytes=64)
            cgs = work.tile([P, 2 * P], U8, tag="cgs", bufs=12, name="cgs", align_bytes=64)
            nc.vector.quantize_mx(out=cgq[:].bitcast(FP8X4), scales=cgs[:], in_=cg[:].rearrange("p m n t -> p (m n t)"))
            return cgq, cgs

        def project(p, mm, codes):
            y, j = divmod(p, 4)
            m = 2 * j + mm
            acc = misc()
            accf = acc[:].rearrange("p m n -> p (m n)")
            cols = slice(P * mm, P * (mm + 1))
            for k in range(3):
                nc.tensor.matmul_mx(out=accf, lhsT=codes[k][0][:, cols].bitcast(FP8X4), lhsT_scale=codes[k][1][:, cols],
                                    rhs=wq[:, k, :].bitcast(FP8X4), rhs_scale=ws[:, k, :], start=(k == 0), stop=(k == 2))
            return p, mm, accf

        def add_disp(p, mm, accf):
            b = 2 * p + mm
            x = work.tile([P, F], F32, tag="x", bufs=3, name="x")
            nc.vector.scalar_tensor_tensor(out=x[:], in0=w_bc[:], scalar=dm1[:, b : b + 1], in1=accf, op0=ALU.mult, op1=ALU.add)
            return x

        def bias_add(x, eng):
            xb = work.tile([P, F], F32, tag="xb", bufs=3, name="xb")
            eng.tensor_tensor(out=xb[:], in0=x[:], in1=b_bc[:], op=ALU.add)
            return xb

        def finish(p, mm, xb):
            y, j = divmod(p, 4)
            m = 2 * j + mm
            o = work.tile([P, F], F32, tag="o", bufs=3, name="o")
            nc.scalar.activation(out=o[:], in_=xb[:], func=ACT.Relu)
            nc.sync.dma_start(out=out[y].rearrange("(p m) f -> p m f", m=MB)[:, m, :], in_=o[:])


        gain_steps = list(gain_steps)
        for t in range(4):
            wide = wide_tile()
            for G in range(2):
                widen(0, t, wide, G)
                for n in range(2):
                    if gain_steps:
                        gain_steps.pop(0)()
            if t == 1:
                turn_pixels(0)
            turn_right(0, t, wide)
        while gain_steps:
            gain_steps.pop(0)()
        flg = turn_left(0, 0)
        turn_slots(0)
        quantise_right(0, 0)
        turn_slots(1)
        quantise_left(0, 0, flg)
        quantise_right(0, 1)
        for k in range(3):
            group_w(k)

        win0, win1, cen, cenw, sqs, ebank, cgs, ps_of, codes = {}, {}, {}, {}, {}, {}, {}, {}, {}

        def e_mm(p, n):
            g, mm = divmod(n, 2)
            ebank[p, n] = window0(p // 4, 2 * (p % 4) + mm, g)

        def e_exp(p, n):
            win0[p, n] = exp0(ebank.pop((p, n)))

        def c_mm(p):
            cen[p], win1[p] = centres(p // 4, p % 4)

        def sq(p, s):
            sqs[p, s] = square1(cen[p], s)

        def ex(p, s):
            exp1(win1[p], sqs.pop((p, s)), s)

        def corr(step):
            p, i = divmod(step, 6)
            k, mm = divmod(i, 2)
            ps_of[step] = correlate(p // 4, 2 * (p % 4) + mm, SLOTS[k])

        def tap(step):
            p, i = divmod(step, 6)
            k, mm = divmod(i, 2)
            if mm == 0:
                cg = work.tile([P, 2, P, 4], BF16, tag="cg%d" % k, bufs=2, name="cg%d" % k, align_bytes=64)
                cgs[p, k] = cg
            win = win1[p][:, :, P * mm : P * (mm + 1)].rearrange("p t n -> p n t") if k == 2 else win0.pop((p, i))[:]
            nc.vector.tensor_tensor(out=cgs[p, k][:, mm], in0=ps_of.pop(step)[:].rearrange("p t n -> p n t"), in1=win, op=ALU.mult)

        def quantise_cg(p, k):
            codes[p, k] = quantise_taps(cgs.pop((p, k)))

        c_mm(0)
        for n in range(4):
            e_mm(0, n)
            e_exp(0, n)
            sq(0, n)
            ex(0, n)
        corr(0)
        corr(1)
        turn_pixels(1)
        c_mm(1)

        wide1, lefts = {}, {}
        acc_at = {14 + (5 * n) // 2: n for n in range(14)}
        acc, xb, xbs = [], [], []
        for step in range(48):
            p, i = divmod(step, 6)
            if p < 7:
                n = {0: 0, 1: 1, 3: 2, 4: 3}.get(i)
                if n is not None:
                    e_mm(p + 1, n)
            if i == 5 and p < 6:
                c_mm(p + 2)
            if step in acc_at:
                q, qm = divmod(acc_at[step], 2)
                acc.append((step, project(q, qm, [codes[q, k] for k in range(3)])))
            if step + 2 < 48:
                corr(step + 2)
            if p < 7 and i == 0:
                lefts[p + 1] = turn_left_mm((p + 1) // 4, (p + 1) % 4)
            if acc and acc[0][0] <= step - 2:
                a = acc.pop(0)[1]
                xb.append((step, a[0], a[1], bias_add(add_disp(*a), nc.gpsimd if step < 44 else nc.vector)))
            tap(step)
            if p and i == 0:
                quantise_cg(p - 1, 2)
            if i == 2:
                quantise_cg(p, 0)
            if i == 4:
                quantise_cg(p, 1)
            if p < 7 and i == 3:
                quantise_left((p + 1) // 4, (p + 1) % 4, lefts.pop(p + 1))
            if p < 2 and i in (1, 4):
                t = 2 * p + i // 3
                wide1[t] = wide_tile()
                widen(1, t, wide1[t], 0)
                widen(1, t, wide1[t], 1)
            if step in (12, 14):
                quantise_right(1, step // 2 - 6)
            if step in (9, 11, 13):
                quantise_w((step - 9) // 2)
            if p < 7:
                if i == 0:
                    sq(p + 1, 0)
                    sq(p + 1, 1)
                if i == 1:
                    e_exp(p + 1, 0)
                    sq(p + 1, 2)
                    sq(p + 1, 3)
                if i == 2:
                    e_exp(p + 1, 1)
                    lefts[p + 1] = copy_left(lefts[p + 1])
                if i == 3:
                    ex(p + 1, 0)
                    ex(p + 1, 1)
                if i == 4:
                    e_exp(p + 1, 2)
                    ex(p + 1, 2)
                if i == 5:
                    e_exp(p + 1, 3)
                    ex(p + 1, 3)
            if p < 2 and i in (2, 5):
                t = 2 * p + i // 5
                turn_right(1, t, wide1[t])
            if step == 5:
                w_bc = spread(wd4, "w_bc", nc.scalar.copy)
                b_bc = spread(bm4, "b_bc", nc.scalar.copy)
                turn_pixels(2)
                turn_pixels(3)
            if xb and xb[0][0] <= step - 2:
                a = xb.pop(0)
                finish(a[1], a[2], a[3])
        quantise_cg(7, 2)
        accs = [project(7, mm, [codes[7, k] for k in range(3)]) for mm in range(2)]
        for s, a in acc:
            xb.append((s, a[0], a[1], bias_add(add_disp(*a), nc.vector)))
        for a in xb:
            finish(a[1], a[2], a[3])
        for a in accs:
            finish(a[0], a[1], bias_add(add_disp(*a), nc.vector))
